import numpy as np
import ml_dtypes


def mxq(x, axis, fmt="e4m3"):
    dtype, down = {"e4m3": (ml_dtypes.float8_e4m3fn, 7), "e5m2": (ml_dtypes.float8_e5m2, 14)}[fmt]
    v = np.moveaxis(np.asarray(x, np.float32).astype(ml_dtypes.bfloat16).astype(np.float64), axis, -1)
    blocks = v.reshape(v.shape[:-1] + (-1, 32))
    amax = np.abs(blocks).max(-1, keepdims=True)
    byte = np.maximum(np.where(amax > 0, np.frexp(amax)[1] - 1 + 127, 0) - down, 1)
    scale = np.exp2(byte - 127.0)
    codes = (blocks / scale).astype(np.float32).astype(dtype).astype(np.float64)
    return np.moveaxis((codes * scale).reshape(v.shape), -1, axis)


WIDE = False


def mx_kscale(k):
    if not WIDE:
        return np.ones(k)
    levels = np.array([10, -10, 5, -5, 0])
    if k % 512:
        return np.exp2(np.random.permutation(np.resize(levels, k // 32))).repeat(32)
    a = np.empty((k // 512, 16))
    for p in range(k // 512):
        a[p, :8] = np.random.permutation(np.resize(levels, 8))
        for g in range(8):
            far = levels[np.abs(levels - a[p, g]) >= 10]
            a[p, g + 8] = far[np.random.randint(len(far))]
    return np.exp2(a.ravel()).repeat(32)


def f64(x):
    return np.asarray(x).astype(np.float64)


def striped(idx):
    return np.tile(np.asarray(idx).reshape(-1, 16).T, (8, 1)).astype(np.uint16)


def unstriped(offs):
    return offs[:16].T.reshape(-1).astype(np.int64)


E2M1 = np.array([0.0, 0.5, 1.0, 1.5, 2.0, 3.0, 4.0, 6.0, -0.0, -0.5, -1.0, -1.5, -2.0, -3.0, -4.0, -6.0])


def pack_weight(w, fmt):
    k, n = w.shape
    w = f64(np.asarray(w, np.float32).astype(ml_dtypes.bfloat16)).reshape(k // 32, 32, n)
    amax = np.abs(w).max(1)
    if fmt == "e4m3":
        byte = np.frexp(amax)[1] - 1 + 127 - 7
    else:
        mant, ex = np.frexp(amax / 6.0)
        byte = np.where(mant > 0.5, ex, ex - 1) + 127
    byte = np.clip(np.where(amax > 0, byte, 1), 1, 254)
    scaled = (w * np.exp2(127.0 - byte)[:, None, :]).reshape(k, n).astype(np.float32)
    by_word = np.ascontiguousarray(scaled.reshape(k // 512, 128, 4, n).transpose(0, 1, 3, 2))
    if fmt == "e4m3":
        words = by_word.astype(ml_dtypes.float8_e4m3fn).view(np.uint8)
    else:
        c = by_word.astype(ml_dtypes.float4_e2m1fn).view(np.uint8) & 0xF
        words = (c[..., 0::2] | (c[..., 1::2] << 4)).reshape(k // 512, 128, 2 * n)
    return np.ascontiguousarray(words), np.ascontiguousarray(byte.astype(np.uint8).reshape(k // 512, 16, n))


def unpack_weight(words, scales, fmt):
    g, _, n = scales.shape
    words = np.ascontiguousarray(words).reshape(g, 128, n, -1)
    if fmt == "e4m3":
        vals = words.view(ml_dtypes.float8_e4m3fn).astype(np.float64)
    else:
        nib = np.empty((g, 128, n, 4), np.uint8)
        nib[..., 0::2] = words & 0xF
        nib[..., 1::2] = words >> 4
        vals = E2M1[nib]
    vals = vals * np.repeat(np.exp2(scales.astype(np.float64) - 127.0), 8, axis=1)[..., None]
    return vals.transpose(0, 1, 3, 2).reshape(g * 512, n)


def bf(x):
    return np.asarray(x, np.float32).astype(ml_dtypes.bfloat16)


def planes(Y):
    r, m = Y.shape
    b = f64(bf(Y)).reshape(r // 32, 32, m)
    amax = np.abs(b).max(1)
    byte = np.clip(np.where(amax > 0, np.frexp(amax)[1] - 1 + 127 - 7, 1), 1, 254)
    codes = (b * np.exp2(127.0 - byte)[:, None, :]).reshape(r, m).astype(np.float32).astype(ml_dtypes.float8_e4m3fn).view(np.uint8)
    words = codes.reshape(r // 512, 128, 4, m).transpose(0, 1, 3, 2)
    return np.ascontiguousarray(words), np.ascontiguousarray(byte.astype(np.uint8).reshape(r // 512, 16, m))


B, N, T, D, NQ = 1, 512, 2048, 512, 512
DV = 512


def sgn(shape):
    return np.random.uniform(0.5, 2.0, shape) * np.where(np.random.standard_normal(shape) < 0, -1.0, 1.0)


def setup_inputs():
    n = np.random.standard_normal
    idx = np.random.permutation(T)[:B * N]
    s = mx_kscale(D)[:, None]
    u = mx_kscale(N)
    ut = np.ones(T)
    ut[idx] = u
    kp = pack_weight(n((D, T)) / s, "e4m3")
    return {
        "qT": (n((B, D, NQ)) * s * (1.00 / np.sqrt(D))).astype(np.float32),
        "k_words": kp[0],
        "k_scales": kp[1],
        "vT": (n((DV, T)) / ut).astype(np.float32),
        "nb": np.tile(0.5 * n(2048), (128, 1)).astype(np.float32),
        "us": (sgn((B, N, 1)) * u[:, None]).astype(np.float32),
        "offs": striped(idx),
    }


def reference(qT, k_words, k_scales, vT, nb, us, offs):
    idx = unstriped(offs)
    pick = lambda x, which: x[:, which].reshape(x.shape[0], B, -1).transpose(1, 0, 2)
    k = unpack_weight(k_words, k_scales, "e4m3")
    kg = pick(k, idx)
    qq = mxq(f64(qT), 1, "e4m3")
    a = kg.transpose(0, 2, 1) @ qq
    y = np.maximum(a + pick(f64(nb), idx)[:, :1, :].transpose(0, 2, 1), 0.0) * f64(us)
    wq = mxq(y, 1, "e4m3")
    o = mxq(pick(f64(vT), idx).transpose(0, 2, 1), 1, "e4m3").transpose(0, 2, 1) @ wq
    Y = o[0]
    words, scales = planes(Y)
    return Y, words, scales

@@ -1,0 +1,184 @@
+from contextlib import ExitStack
+
+import concourse.mybir as mybir
+from concourse.masks import make_identity
+
+F32 = mybir.dt.float32
+BF16 = mybir.dt.bfloat16
+I32 = mybir.dt.int32
+U32 = mybir.dt.uint32
+U16 = mybir.dt.uint16
+U8 = mybir.dt.uint8
+FP8X4 = mybir.dt.float8_e4m3fn_x4
+ACT = mybir.ActivationFunctionType
+ALU = mybir.AluOpType
+
+P = 128
+PACK = 4
+SLOTS = 512
+POOL = 2048
+NQ = 512
+HALF = NQ // 2
+
+FLOPS = 2 * 2 * 512 * 512 * 512
+
+
+def tile_attend_plo_mlprelu_topk_kernel(tc, qT, k_words, k_scales, vT, nb, us, offs, out_0, out_1, out_2):
+    nc = tc.nc
+    with ExitStack() as ctx:
+        held = ctx.enter_context(tc.tile_pool(name="held", bufs=1))
+        shared = ctx.enter_context(tc.tile_pool(name="shared", bufs=1))
+        psum = ctx.enter_context(tc.psum_pool(name="psum", bufs=1))
+
+        def sb(name, shape, dtype):
+            return held.tile(shape, dtype, name=name, align_bytes=64)
+
+        def bank(b, shape, name):
+            return psum.tile(shape, F32, name=name, tag="bank%d" % b)
+
+        offsets = held.tile([P, SLOTS // 16], U16, name="offsets")
+        nc.sync.dma_start(offsets[:], offs)
+
+        k_scale_pool = sb("k_scale_pool", [P, POOL], U8)
+        nb_pool = sb("nb_pool", [P, POOL], F32)
+        nc.gpsimd.memset(k_scale_pool[:].bitcast(I32), 0)
+        nc.vector.memset(nb_pool[0 : P - 1, :], 0.0)
+
+        q_raw = sb("q_raw", [P, PACK, NQ], F32)
+        nc.sync.dma_start(q_raw[:], qT[0].rearrange("(p t) q -> p t q", t=PACK))
+        us_sb = sb("us_sb", [P, PACK], F32)
+        nc.scalar.dma_start(nb_pool[P - 1 : P, :], nb[0:1, :])
+        nc.scalar.dma_start(us_sb[:], us[0].rearrange("(p t) o -> p (t o)", t=PACK))
+        for quad in range(4):
+            nc.sync.dma_start(
+                k_scale_pool[32 * quad : 32 * quad + 4, :].bitcast(I32),
+                k_scales[0, 4 * quad : 4 * quad + 4, :].bitcast(I32),
+            )
+        k_word_pool = sb("k_word_pool", [P, POOL], I32)
+        nc.sync.dma_start(k_word_pool[:], k_words[0].rearrange("p n t -> p (n t)").bitcast(I32))
+        v_rows = vT.rearrange("(p j) n -> p j n", j=PACK)
+        v_pool = [sb("v_pool%d" % j, [P, POOL], F32) for j in range(PACK)]
+        for j in range(PACK):
+            nc.sync.dma_start(v_pool[j][:], v_rows[:, j, :])
+
+        ident = sb("ident", [P, P], F32)
+        make_identity(nc, ident[:])
+
+        us_abs = sb("us_abs", [P, PACK], F32)
+        us_sign = sb("us_sign", [P, PACK], F32)
+        nc.scalar.activation(us_abs[:], us_sb[:], ACT.Abs)
+        nc.scalar.activation(us_sign[:], us_sb[:], ACT.Sign)
+
+        nb_g = sb("nb_g", [P, SLOTS], F32)
+        nc.vector.tensor_copy(nb_g[:], nb_pool[:].indirect(offsets[:]))
+        nb_t = bank(7, [P, PACK, P], "nb_t")
+        for t in range(PACK):
+            nc.tensor.transpose(nb_t[:, t, :], nb_g[:, t:SLOTS:PACK], ident[:])
+
+        ks_g = sb("ks_g", [P, SLOTS], U8)
+        nc.vector.tensor_copy(ks_g[:], k_scale_pool[:].indirect(offsets[:]))
+        ks = sb("ks", [P, PACK, P], U8)
+        nc.vector.tensor_copy(ks[:].rearrange("p t s -> p s t"), ks_g[:].rearrange("p (s t) -> p s t", t=PACK))
+
+        bias = sb("bias", [P, PACK], F32)
+        nc.vector.tensor_tensor(bias[:], nb_t[:, :, P - 1], us_abs[:], ALU.mult)
+
+        q_codes = sb("q_codes", [P, NQ], U32)
+        q_scales = sb("q_scales", [P, NQ], U8)
+        q_grp = [sb("q_grp%d" % h, [P, HALF, PACK], BF16) for h in range(2)]
+        nc.scalar.copy(q_grp[0][:], q_raw[:, :, 0:HALF].rearrange("p t q -> p q t"))
+        nc.vector.tensor_copy(q_grp[1][:], q_raw[:, :, HALF:NQ].rearrange("p t q -> p q t"))
+        for h in (1, 0):
+            cols = slice(h * HALF, (h + 1) * HALF)
+            nc.vector.quantize_mx(
+                out=q_codes[:, cols].bitcast(FP8X4), scales=q_scales[:, cols], in_=q_grp[h][:].rearrange("p q t -> p (q t)")
+            )
+
+        kw = sb("kw", [P, PACK, P], U32)
+        nc.vector.tensor_copy(kw[:].rearrange("p t s -> p s t"), k_word_pool[:].bitcast(U32).indirect(offsets[:]))
+
+        y_abs = [shared.tile([P, NQ], BF16, name="y_abs%d" % t, offset=4096 + 1024 * t, align_bytes=64) for t in range(PACK)]
+        y_pl = sb("y_pl", [P, PACK, NQ], BF16)
+        for t in range(PACK):
+            a = bank(t, [P, NQ], "a%d" % t)
+            nc.tensor.matmul_mx(
+                out=a[:], lhsT=kw[:, t, :].bitcast(FP8X4), lhsT_scale=ks[:, t, :],
+                rhs=q_codes[:].bitcast(FP8X4), rhs_scale=q_scales[:], start=True, stop=True,
+            )
+            nc.scalar.activation(y_abs[t][:], a[:], ACT.Relu, bias=bias[:, t : t + 1], scale=us_abs[:, t : t + 1])
+
+        v_codes = [sb("v_codes%d" % j, [P, P], U32) for j in range(PACK)]
+        v_scales = [sb("v_scales%d" % j, [P, P], U8) for j in range(PACK)]
+        v_grp = [sb("v_grp%d" % j, [P, P, PACK], BF16) for j in range(PACK)]
+
+        def gather_and_turn(j):
+            v_g = shared.tile([P, SLOTS], BF16, name="v_g%d" % j, offset=(8192, 7168, 0, 1024)[j], align_bytes=64)
+            nc.vector.tensor_copy(v_g[:], v_pool[j][:].indirect(offsets[:]))
+            pairs = v_g[:].bitcast(F32)
+            turned = bank(3 + j, [P, 2, P], "turned%d" % j)
+            for u in range(2):
+                nc.tensor.transpose(turned[:, u, :], pairs[:, u : SLOTS // 2 : 2], ident[:])
+            nc.scalar.copy(v_grp[j][:].bitcast(F32), turned[:].rearrange("p u e -> p e u"))
+
+        def quantise_v(j):
+            nc.vector.quantize_mx(
+                out=v_codes[j][:].bitcast(FP8X4), scales=v_scales[j][:], in_=v_grp[j][:].rearrange("p e t -> p (e t)")
+            )
+
+        gather_and_turn(0)
+        for t in range(PACK):
+            nc.vector.tensor_scalar(y_pl[:, t, :], y_abs[t][:], us_sign[:, t : t + 1], None, ALU.mult)
+        gather_and_turn(1)
+        y_grp = shared.tile([P, NQ, PACK], BF16, name="y_grp", offset=0, align_bytes=64)
+        nc.vector.tensor_copy(y_grp[:], y_pl[:].rearrange("p t q -> p q t"))
+        quantise_v(0)
+        y_codes = sb("y_codes", [P, NQ], U32)
+        y_scales = sb("y_scales", [P, NQ], U8)
+        nc.vector.quantize_mx(out=y_codes[:].bitcast(FP8X4), scales=y_scales[:], in_=y_grp[:].rearrange("p q t -> p (q t)"))
+        quantise_v(1)
+        o_sb = sb("o_sb", [P, PACK, NQ], F32)
+        out_rows = out_0.rearrange("(p j) q -> p j q", j=PACK)
+
+        def product(j, b, cols, name):
+            o = bank(b, [P, cols.stop - cols.start], name)
+            nc.tensor.matmul_mx(
+                out=o[:], lhsT=v_codes[j][:].bitcast(FP8X4), lhsT_scale=v_scales[j][:],
+                rhs=y_codes[:, cols].bitcast(FP8X4), rhs_scale=y_scales[:, cols], start=True, stop=True,
+            )
+            nc.scalar.copy(o_sb[:, j, cols], o[:])
+
+        def whole(j):
+            product(j, j, slice(0, NQ), "o%d" % j)
+            nc.sync.dma_start(out_rows[:, j, :], o_sb[:, j, :])
+
+        whole(0)
+        whole(1)
+        gather_and_turn(2)
+        gather_and_turn(3)
+        quantise_v(2)
+        whole(2)
+        quantise_v(3)
+        last = PACK - 1
+        product(last, 3, slice(0, HALF), "o3a")
+        product(last, 7, slice(HALF, NQ), "o3b")
+        nc.sync.dma_start(out_rows[:, last, :], o_sb[:, last, :])
+
+        o_codes = sb("o_codes", [P, NQ], U32)
+        o_scales = sb("o_scales", [P, NQ], U8)
+        o_grp = [sb("o_grp%d" % h, [P, HALF, PACK], BF16) for h in range(2)]
+        words = out_1[0].rearrange("p n t -> p (n t)").bitcast(I32)
+        for h in range(2):
+            cols = slice(h * HALF, (h + 1) * HALF)
+            nc.vector.tensor_copy(o_grp[h][:], o_sb[:, :, cols].rearrange("p j q -> p q j"))
+        for h in range(2):
+            cols = slice(h * HALF, (h + 1) * HALF)
+            nc.vector.quantize_mx(
+                out=o_codes[:, cols].bitcast(FP8X4), scales=o_scales[:, cols], in_=o_grp[h][:].rearrange("p q j -> p (q j)")
+            )
+            nc.sync.dma_start(words[:, cols], o_codes[:, cols].bitcast(I32))
+        for quad in range(4):
+            eng = nc.scalar if quad % 2 else nc.sync
+            eng.dma_start(
+                out_2[0, 4 * quad : 4 * quad + 4, :].bitcast(I32),
+                o_scales[32 * quad : 32 * quad + 4, :].bitcast(I32),
+            )

@@ -33,6 +33,9 @@ def tile_attend_plo_mlprelu_topk_kernel(tc, qT, k_words, k_scales, vT, nb, us, o
         def sb(name, shape, dtype):
             return held.tile(shape, dtype, name=name, align_bytes=64)
 
+        def over(name, shape, dtype, offset):
+            return shared.tile(shape, dtype, name=name, offset=offset, align_bytes=64)
+
         def bank(b, shape, name):
             return psum.tile(shape, F32, name=name, tag="bank%d" % b)
 
@@ -44,20 +47,20 @@ def tile_attend_plo_mlprelu_topk_kernel(tc, qT, k_words, k_scales, vT, nb, us, o
         nc.gpsimd.memset(k_scale_pool[:].bitcast(I32), 0)
         nc.vector.memset(nb_pool[0 : P - 1, :], 0.0)
 
-        q_raw = sb("q_raw", [P, PACK, NQ], F32)
-        nc.sync.dma_start(q_raw[:], qT[0].rearrange("(p t) q -> p t q", t=PACK))
         us_sb = sb("us_sb", [P, PACK], F32)
+        nc.sync.dma_start(us_sb[:], us[0].rearrange("(p t) o -> p (t o)", t=PACK))
         nc.scalar.dma_start(nb_pool[P - 1 : P, :], nb[0:1, :])
-        nc.scalar.dma_start(us_sb[:], us[0].rearrange("(p t) o -> p (t o)", t=PACK))
         for quad in range(4):
-            nc.sync.dma_start(
+            (nc.sync if quad < 2 else nc.scalar).dma_start(
                 k_scale_pool[32 * quad : 32 * quad + 4, :].bitcast(I32),
                 k_scales[0, 4 * quad : 4 * quad + 4, :].bitcast(I32),
             )
+        q_raw = sb("q_raw", [P, PACK, NQ], F32)
+        nc.sync.dma_start(q_raw[:], qT[0].rearrange("(p t) q -> p t q", t=PACK))
         k_word_pool = sb("k_word_pool", [P, POOL], I32)
         nc.sync.dma_start(k_word_pool[:], k_words[0].rearrange("p n t -> p (n t)").bitcast(I32))
         v_rows = vT.rearrange("(p j) n -> p j n", j=PACK)
-        v_pool = [sb("v_pool%d" % j, [P, POOL], F32) for j in range(PACK)]
+        v_pool = [over("v_pool%d" % j, [P, POOL], F32, 8192 * j) for j in range(PACK)]
         for j in range(PACK):
             nc.sync.dma_start(v_pool[j][:], v_rows[:, j, :])
 
@@ -75,21 +78,20 @@ def tile_attend_plo_mlprelu_topk_kernel(tc, qT, k_words, k_scales, vT, nb, us, o
         for t in range(PACK):
             nc.tensor.transpose(nb_t[:, t, :], nb_g[:, t:SLOTS:PACK], ident[:])
 
-        ks_g = sb("ks_g", [P, SLOTS], U8)
+        ks_g = over("ks_g", [P, SLOTS], U8, 34560)
         nc.vector.tensor_copy(ks_g[:], k_scale_pool[:].indirect(offsets[:]))
         ks = sb("ks", [P, PACK, P], U8)
         nc.vector.tensor_copy(ks[:].rearrange("p t s -> p s t"), ks_g[:].rearrange("p (s t) -> p s t", t=PACK))
 
-        bias = sb("bias", [P, PACK], F32)
+        bias = over("bias", [P, PACK], F32, 34816)
         nc.vector.tensor_tensor(bias[:], nb_t[:, :, P - 1], us_abs[:], ALU.mult)
 
-        q_codes = sb("q_codes", [P, NQ], U32)
+        q_codes = over("q_codes", [P, NQ], U32, 32768)
         q_scales = sb("q_scales", [P, NQ], U8)
         q_grp = [sb("q_grp%d" % h, [P, HALF, PACK], BF16) for h in range(2)]
-        nc.scalar.copy(q_grp[0][:], q_raw[:, :, 0:HALF].rearrange("p t q -> p q t"))
-        nc.vector.tensor_copy(q_grp[1][:], q_raw[:, :, HALF:NQ].rearrange("p t q -> p q t"))
-        for h in (1, 0):
+        for h in range(2):
             cols = slice(h * HALF, (h + 1) * HALF)
+            nc.scalar.copy(q_grp[h][:], q_raw[:, :, cols].rearrange("p t q -> p q t"))
             nc.vector.quantize_mx(
                 out=q_codes[:, cols].bitcast(FP8X4), scales=q_scales[:, cols], in_=q_grp[h][:].rearrange("p q t -> p (q t)")
             )
@@ -97,8 +99,8 @@ def tile_attend_plo_mlprelu_topk_kernel(tc, qT, k_words, k_scales, vT, nb, us, o
         kw = sb("kw", [P, PACK, P], U32)
         nc.vector.tensor_copy(kw[:].rearrange("p t s -> p s t"), k_word_pool[:].bitcast(U32).indirect(offsets[:]))
 
-        y_abs = [shared.tile([P, NQ], BF16, name="y_abs%d" % t, offset=4096 + 1024 * t, align_bytes=64) for t in range(PACK)]
-        y_pl = sb("y_pl", [P, PACK, NQ], BF16)
+        y_abs = [sb("y_abs%d" % t, [P, NQ], BF16) for t in range(PACK)]
+        y_pl = over("y_pl", [P, PACK, NQ], BF16, 0)
         for t in range(PACK):
             a = bank(t, [P, NQ], "a%d" % t)
             nc.tensor.matmul_mx(
@@ -107,12 +109,14 @@ def tile_attend_plo_mlprelu_topk_kernel(tc, qT, k_words, k_scales, vT, nb, us, o
             )
             nc.scalar.activation(y_abs[t][:], a[:], ACT.Relu, bias=bias[:, t : t + 1], scale=us_abs[:, t : t + 1])
 
-        v_codes = [sb("v_codes%d" % j, [P, P], U32) for j in range(PACK)]
+        v_codes = [over("v_codes%d" % j, [P, P], U32, (12288, 36864, 24576, 37376)[j]) for j in range(PACK)]
         v_scales = [sb("v_scales%d" % j, [P, P], U8) for j in range(PACK)]
         v_grp = [sb("v_grp%d" % j, [P, P, PACK], BF16) for j in range(PACK)]
 
+        v_gs = {}
+
         def gather_and_turn(j):
-            v_g = shared.tile([P, SLOTS], BF16, name="v_g%d" % j, offset=(8192, 7168, 0, 1024)[j], align_bytes=64)
+            v_g = v_gs[j] = sb("v_g%d" % j, [P, SLOTS], BF16)
             nc.vector.tensor_copy(v_g[:], v_pool[j][:].indirect(offsets[:]))
             pairs = v_g[:].bitcast(F32)
             turned = bank(3 + j, [P, 2, P], "turned%d" % j)
@@ -129,12 +133,17 @@ def tile_attend_plo_mlprelu_topk_kernel(tc, qT, k_words, k_scales, vT, nb, us, o
         for t in range(PACK):
             nc.vector.tensor_scalar(y_pl[:, t, :], y_abs[t][:], us_sign[:, t : t + 1], None, ALU.mult)
         gather_and_turn(1)
-        y_grp = shared.tile([P, NQ, PACK], BF16, name="y_grp", offset=0, align_bytes=64)
-        nc.vector.tensor_copy(y_grp[:], y_pl[:].rearrange("p t q -> p q t"))
+        y_grp = [sb("y_grp0", [P, HALF, PACK], BF16), over("y_grp1", [P, HALF, PACK], BF16, 8192)]
+        nc.scalar.copy(y_grp[0][:], y_pl[:, :, 0:HALF].rearrange("p t q -> p q t"))
+        nc.vector.tensor_copy(y_grp[1][:], y_pl[:, :, HALF:NQ].rearrange("p t q -> p q t"))
         quantise_v(0)
-        y_codes = sb("y_codes", [P, NQ], U32)
+        y_codes = over("y_codes", [P, NQ], U32, 10240)
         y_scales = sb("y_scales", [P, NQ], U8)
-        nc.vector.quantize_mx(out=y_codes[:].bitcast(FP8X4), scales=y_scales[:], in_=y_grp[:].rearrange("p q t -> p (q t)"))
+        for h in range(2):
+            cols = slice(h * HALF, (h + 1) * HALF)
+            nc.vector.quantize_mx(
+                out=y_codes[:, cols].bitcast(FP8X4), scales=y_scales[:, cols], in_=y_grp[h][:].rearrange("p q t -> p (q t)")
+            )
         quantise_v(1)
         o_sb = sb("o_sb", [P, PACK, NQ], F32)
         out_rows = out_0.rearrange("(p j) q -> p j q", j=PACK)
@@ -149,7 +158,7 @@ def tile_attend_plo_mlprelu_topk_kernel(tc, qT, k_words, k_scales, vT, nb, us, o
 
         def whole(j):
             product(j, j, slice(0, NQ), "o%d" % j)
-            nc.sync.dma_start(out_rows[:, j, :], o_sb[:, j, :])
+            (nc.scalar if j < 2 else nc.sync).dma_start(out_rows[:, j, :], o_sb[:, j, :])
 
         whole(0)
         whole(1)

@@ -15,179 +15,215 @@ ALU = mybir.AluOpType
 
 P = 128
 PACK = 4
+QUADRANTS = 4
 SLOTS = 512
-POOL = 2048
+NEURONS = 2048
 NQ = 512
 HALF = NQ // 2
+RUN = 4
+POOL_BYTES = NEURONS * 4
+SECOND_TENANT = 2048
+LAST = PACK - 1
 
-FLOPS = 2 * 2 * 512 * 512 * 512
+TURN_BANKS = (4, 5, 6)
+BIAS_BANK = 7
+TAIL_BANKS = (3, 7, 5, 6)
+
+FLOPS = 2 * (2 * 512 * SLOTS * NQ)
 
 
 def tile_attend_plo_mlprelu_topk_kernel(tc, qT, k_words, k_scales, vT, nb, us, offs, out_0, out_1, out_2):
     nc = tc.nc
+    halves = [slice(h * HALF, (h + 1) * HALF) for h in range(2)]
+    quarters = [slice(c * P, (c + 1) * P) for c in range(NQ // P)]
+
     with ExitStack() as ctx:
         held = ctx.enter_context(tc.tile_pool(name="held", bufs=1))
-        shared = ctx.enter_context(tc.tile_pool(name="shared", bufs=1))
+        reused = ctx.enter_context(tc.tile_pool(name="reused", bufs=1))
         psum = ctx.enter_context(tc.psum_pool(name="psum", bufs=1))
 
-        def sb(name, shape, dtype):
+        def own(name, shape, dtype):
             return held.tile(shape, dtype, name=name, align_bytes=64)
 
-        def over(name, shape, dtype, offset):
-            return shared.tile(shape, dtype, name=name, offset=offset, align_bytes=64)
+        def placed(name, shape, dtype, offset):
+            return reused.tile(shape, dtype, name=name, offset=offset, align_bytes=64)
 
         def bank(b, shape, name):
             return psum.tile(shape, F32, name=name, tag="bank%d" % b)
 
+        def weave(copy, grouped, planes):
+            copy(grouped.rearrange("p (c i) t -> p c t i", i=RUN), planes.rearrange("p t (c i) -> p c t i", i=RUN))
+
+        def quantise(codes, scales, grouped):
+            nc.vector.quantize_mx(out=codes.bitcast(FP8X4), scales=scales, in_=grouped.rearrange("p c t -> p (c t)"))
+
+        def product(acc, left, left_scales, right, right_scales):
+            nc.tensor.matmul_mx(
+                out=acc,
+                lhsT=left.bitcast(FP8X4),
+                lhsT_scale=left_scales,
+                rhs=right.bitcast(FP8X4),
+                rhs_scale=right_scales,
+                start=True,
+                stop=True,
+            )
+
         offsets = held.tile([P, SLOTS // 16], U16, name="offsets")
         nc.sync.dma_start(offsets[:], offs)
 
-        k_scale_pool = sb("k_scale_pool", [P, POOL], U8)
-        nb_pool = sb("nb_pool", [P, POOL], F32)
+        k_scale_pool = own("k_scale_pool", [P, NEURONS], U8)
+        nb_pool = own("nb_pool", [P, NEURONS], F32)
         nc.gpsimd.memset(k_scale_pool[:].bitcast(I32), 0)
         nc.vector.memset(nb_pool[0 : P - 1, :], 0.0)
 
-        us_sb = sb("us_sb", [P, PACK], F32)
+        us_sb = own("us_sb", [P, PACK], F32)
         nc.sync.dma_start(us_sb[:], us[0].rearrange("(p t) o -> p (t o)", t=PACK))
         nc.scalar.dma_start(nb_pool[P - 1 : P, :], nb[0:1, :])
-        for quad in range(4):
-            (nc.sync if quad < 2 else nc.scalar).dma_start(
+        for quad in range(QUADRANTS):
+            queue = nc.sync if quad < QUADRANTS // 2 else nc.scalar
+            queue.dma_start(
                 k_scale_pool[32 * quad : 32 * quad + 4, :].bitcast(I32),
                 k_scales[0, 4 * quad : 4 * quad + 4, :].bitcast(I32),
             )
-        q_raw = sb("q_raw", [P, PACK, NQ], F32)
-        nc.sync.dma_start(q_raw[:], qT[0].rearrange("(p t) q -> p t q", t=PACK))
-        k_word_pool = sb("k_word_pool", [P, POOL], I32)
+        q_planes = own("q_planes", [P, PACK, NQ], F32)
+        nc.sync.dma_start(q_planes[:], qT[0].rearrange("(p t) q -> p t q", t=PACK))
+        k_word_pool = own("k_word_pool", [P, NEURONS], I32)
         nc.sync.dma_start(k_word_pool[:], k_words[0].rearrange("p n t -> p (n t)").bitcast(I32))
         v_rows = vT.rearrange("(p j) n -> p j n", j=PACK)
-        v_pool = [over("v_pool%d" % j, [P, POOL], F32, 8192 * j) for j in range(PACK)]
+        v_pool = [placed("v_pool%d" % j, [P, NEURONS], F32, POOL_BYTES * j) for j in range(PACK)]
         for j in range(PACK):
             nc.sync.dma_start(v_pool[j][:], v_rows[:, j, :])
 
-        ident = sb("ident", [P, P], F32)
+        ident = own("ident", [P, P], F32)
         make_identity(nc, ident[:])
 
-        us_abs = sb("us_abs", [P, PACK], F32)
-        us_sign = sb("us_sign", [P, PACK], F32)
+        us_abs = own("us_abs", [P, PACK], F32)
+        us_sign = own("us_sign", [P, PACK], F32)
         nc.scalar.activation(us_abs[:], us_sb[:], ACT.Abs)
         nc.scalar.activation(us_sign[:], us_sb[:], ACT.Sign)
 
-        nb_g = sb("nb_g", [P, SLOTS], F32)
-        nc.vector.tensor_copy(nb_g[:], nb_pool[:].indirect(offsets[:]))
-        nb_t = bank(7, [P, PACK, P], "nb_t")
+        nb_listed = own("nb_listed", [P, SLOTS], F32)
+        nc.vector.tensor_copy(nb_listed[:], nb_pool[:].indirect(offsets[:]))
+        nb_turned = bank(BIAS_BANK, [P, PACK, P], "nb_turned")
         for t in range(PACK):
-            nc.tensor.transpose(nb_t[:, t, :], nb_g[:, t:SLOTS:PACK], ident[:])
+            nc.tensor.transpose(nb_turned[:, t, :], nb_listed[:, t:SLOTS:PACK], ident[:])
 
-        ks_g = over("ks_g", [P, SLOTS], U8, 34560)
-        nc.vector.tensor_copy(ks_g[:], k_scale_pool[:].indirect(offsets[:]))
-        ks = sb("ks", [P, PACK, P], U8)
-        nc.vector.tensor_copy(ks[:].rearrange("p t s -> p s t"), ks_g[:].rearrange("p (s t) -> p s t", t=PACK))
+        k_scales_listed = own("k_scales_listed", [P, SLOTS], U8)
+        nc.vector.tensor_copy(k_scales_listed[:], k_scale_pool[:].indirect(offsets[:]))
+        bias = own("bias", [P, PACK], F32)
+        nc.vector.tensor_tensor(bias[:], nb_turned[:, :, P - 1], us_abs[:], ALU.mult)
+        k_scales_dealt = own("k_scales_dealt", [P, PACK, P], U8)
+        nc.vector.tensor_copy(
+            k_scales_dealt[:].rearrange("p t s -> p s t"), k_scales_listed[:].rearrange("p (s t) -> p s t", t=PACK)
+        )
 
-        bias = over("bias", [P, PACK], F32, 34816)
-        nc.vector.tensor_tensor(bias[:], nb_t[:, :, P - 1], us_abs[:], ALU.mult)
-
-        q_codes = over("q_codes", [P, NQ], U32, 32768)
-        q_scales = sb("q_scales", [P, NQ], U8)
-        q_grp = [sb("q_grp%d" % h, [P, HALF, PACK], BF16) for h in range(2)]
+        q_codes = own("q_codes", [P, NQ], U32)
+        q_scales = own("q_scales", [P, NQ], U8)
+        q_grouped = [own("q_grouped%d" % h, [P, HALF, PACK], BF16) for h in range(2)]
+        weave(nc.scalar.copy, q_grouped[0][:], q_planes[:, :, halves[0]])
+        weave(nc.vector.tensor_copy, q_grouped[1][:], q_planes[:, :, halves[1]])
         for h in range(2):
-            cols = slice(h * HALF, (h + 1) * HALF)
-            nc.scalar.copy(q_grp[h][:], q_raw[:, :, cols].rearrange("p t q -> p q t"))
-            nc.vector.quantize_mx(
-                out=q_codes[:, cols].bitcast(FP8X4), scales=q_scales[:, cols], in_=q_grp[h][:].rearrange("p q t -> p (q t)")
-            )
+            quantise(q_codes[:, halves[h]], q_scales[:, halves[h]], q_grouped[h][:])
 
-        kw = sb("kw", [P, PACK, P], U32)
-        nc.vector.tensor_copy(kw[:].rearrange("p t s -> p s t"), k_word_pool[:].bitcast(U32).indirect(offsets[:]))
+        k_words_dealt = own("k_words_dealt", [P, PACK, P], U32)
+        nc.vector.tensor_copy(
+            k_words_dealt[:].rearrange("p t s -> p s t"), k_word_pool[:].bitcast(U32).indirect(offsets[:])
+        )
 
-        y_abs = [sb("y_abs%d" % t, [P, NQ], BF16) for t in range(PACK)]
-        y_pl = over("y_pl", [P, PACK, NQ], BF16, 0)
+        y_abs = [own("y_abs%d" % t, [P, NQ], BF16) for t in range(PACK)]
         for t in range(PACK):
-            a = bank(t, [P, NQ], "a%d" % t)
-            nc.tensor.matmul_mx(
-                out=a[:], lhsT=kw[:, t, :].bitcast(FP8X4), lhsT_scale=ks[:, t, :],
-                rhs=q_codes[:].bitcast(FP8X4), rhs_scale=q_scales[:], start=True, stop=True,
+            scores = bank(t, [P, NQ], "scores%d" % t)
+            product(scores[:], k_words_dealt[:, t, :], k_scales_dealt[:, t, :], q_codes[:], q_scales[:])
+            nc.scalar.activation(
+                y_abs[t][:], scores[:], ACT.Relu, bias=bias[:, t : t + 1], scale=us_abs[:, t : t + 1]
             )
-            nc.scalar.activation(y_abs[t][:], a[:], ACT.Relu, bias=bias[:, t : t + 1], scale=us_abs[:, t : t + 1])
 
-        v_codes = [over("v_codes%d" % j, [P, P], U32, (12288, 36864, 24576, 37376)[j]) for j in range(PACK)]
-        v_scales = [sb("v_scales%d" % j, [P, P], U8) for j in range(PACK)]
-        v_grp = [sb("v_grp%d" % j, [P, P, PACK], BF16) for j in range(PACK)]
-
-        v_gs = {}
+        v_codes = [placed("v_codes%d" % j, [P, P], U32, POOL_BYTES * (j + 1)) for j in range(LAST)]
+        v_codes.append(own("v_codes%d" % LAST, [P, P], U32))
+        v_scales = [own("v_scales%d" % j, [P, P], U8) for j in range(PACK)]
+        v_grouped = [own("v_grouped%d" % j, [P, P, PACK], BF16) for j in range(LAST)]
+        v_grouped.append(placed("v_grouped%d" % LAST, [P, P, PACK], BF16, POOL_BYTES * PACK))
 
         def gather_and_turn(j):
-            v_g = v_gs[j] = sb("v_g%d" % j, [P, SLOTS], BF16)
-            nc.vector.tensor_copy(v_g[:], v_pool[j][:].indirect(offsets[:]))
-            pairs = v_g[:].bitcast(F32)
-            turned = bank(3 + j, [P, 2, P], "turned%d" % j)
+            listed = own("v_listed%d" % j, [P, SLOTS], BF16)
+            nc.vector.tensor_copy(listed[:], v_pool[j][:].indirect(offsets[:]))
+            pairs = listed[:].bitcast(F32)
+            turned = bank(TURN_BANKS[j % len(TURN_BANKS)], [P, 2, P], "v_turned%d" % j)
             for u in range(2):
                 nc.tensor.transpose(turned[:, u, :], pairs[:, u : SLOTS // 2 : 2], ident[:])
-            nc.scalar.copy(v_grp[j][:].bitcast(F32), turned[:].rearrange("p u e -> p e u"))
+            nc.scalar.copy(v_grouped[j][:].bitcast(F32), turned[:].rearrange("p u e -> p e u"))
 
         def quantise_v(j):
-            nc.vector.quantize_mx(
-                out=v_codes[j][:].bitcast(FP8X4), scales=v_scales[j][:], in_=v_grp[j][:].rearrange("p e t -> p (e t)")
-            )
+            quantise(v_codes[j][:], v_scales[j][:], v_grouped[j][:])
 
         gather_and_turn(0)
+        y_planes = placed("y_planes", [P, PACK, NQ], BF16, 0)
         for t in range(PACK):
-            nc.vector.tensor_scalar(y_pl[:, t, :], y_abs[t][:], us_sign[:, t : t + 1], None, ALU.mult)
+            nc.vector.tensor_scalar(y_planes[:, t, :], y_abs[t][:], us_sign[:, t : t + 1], None, ALU.mult)
         gather_and_turn(1)
-        y_grp = [sb("y_grp0", [P, HALF, PACK], BF16), over("y_grp1", [P, HALF, PACK], BF16, 8192)]
-        nc.scalar.copy(y_grp[0][:], y_pl[:, :, 0:HALF].rearrange("p t q -> p q t"))
-        nc.vector.tensor_copy(y_grp[1][:], y_pl[:, :, HALF:NQ].rearrange("p t q -> p q t"))
+        y_grouped = own("y_grouped", [P, NQ, PACK], BF16)
+        weave(nc.scalar.copy, y_grouped[:], y_planes[:])
         quantise_v(0)
-        y_codes = over("y_codes", [P, NQ], U32, 10240)
-        y_scales = sb("y_scales", [P, NQ], U8)
-        for h in range(2):
-            cols = slice(h * HALF, (h + 1) * HALF)
-            nc.vector.quantize_mx(
-                out=y_codes[:, cols].bitcast(FP8X4), scales=y_scales[:, cols], in_=y_grp[h][:].rearrange("p q t -> p (q t)")
-            )
+        gather_and_turn(2)
+        y_codes = placed("y_codes", [P, NQ], U32, POOL_BYTES * 2 + SECOND_TENANT)
+        y_scales = own("y_scales", [P, NQ], U8)
+        quantise(y_codes[:], y_scales[:], y_grouped[:])
         quantise_v(1)
-        o_sb = sb("o_sb", [P, PACK, NQ], F32)
+
+        o_planes = own("o_planes", [P, PACK, NQ], F32)
         out_rows = out_0.rearrange("(p j) q -> p j q", j=PACK)
 
-        def product(j, b, cols, name):
-            o = bank(b, [P, cols.stop - cols.start], name)
-            nc.tensor.matmul_mx(
-                out=o[:], lhsT=v_codes[j][:].bitcast(FP8X4), lhsT_scale=v_scales[j][:],
-                rhs=y_codes[:, cols].bitcast(FP8X4), rhs_scale=y_scales[:, cols], start=True, stop=True,
-            )
-            nc.scalar.copy(o_sb[:, j, cols], o[:])
+        def result(j, b, cols):
+            acc = bank(b, [P, cols.stop - cols.start], "result%d_%d" % (j, b))
+            product(acc[:], v_codes[j][:], v_scales[j][:], y_codes[:, cols], y_scales[:, cols])
+            nc.scalar.copy(o_planes[:, j, cols], acc[:])
 
-        def whole(j):
-            product(j, j, slice(0, NQ), "o%d" % j)
-            (nc.scalar if j < 2 else nc.sync).dma_start(out_rows[:, j, :], o_sb[:, j, :])
+        def whole_plane(j):
+            result(j, j, slice(0, NQ))
+            nc.sync.dma_start(out_rows[:, j, :], o_planes[:, j, :])
 
-        whole(0)
-        whole(1)
-        gather_and_turn(2)
-        gather_and_turn(3)
+        whole_plane(0)
+        whole_plane(1)
+        gather_and_turn(LAST)
         quantise_v(2)
-        whole(2)
-        quantise_v(3)
-        last = PACK - 1
-        product(last, 3, slice(0, HALF), "o3a")
-        product(last, 7, slice(HALF, NQ), "o3b")
-        nc.sync.dma_start(out_rows[:, last, :], o_sb[:, last, :])
 
-        o_codes = sb("o_codes", [P, NQ], U32)
-        o_scales = sb("o_scales", [P, NQ], U8)
-        o_grp = [sb("o_grp%d" % h, [P, HALF, PACK], BF16) for h in range(2)]
+        o_grouped = [placed("o_grouped0", [P, HALF, PACK], BF16, POOL_BYTES * LAST + SECOND_TENANT)]
+        weave(nc.vector.tensor_copy, o_grouped[0][:, :, 0:2], o_planes[:, 0:2, halves[0]])
+        whole_plane(2)
+        quantise_v(LAST)
+        o_grouped.append(placed("o_grouped1", [P, HALF, PACK], BF16, POOL_BYTES * PACK))
+        weave(nc.vector.tensor_copy, o_grouped[1][:, :, 0:2], o_planes[:, 0:2, halves[1]])
+
+        for c in range(len(quarters)):
+            result(LAST, TAIL_BANKS[c], quarters[c])
+        nc.sync.dma_start(out_rows[:, LAST, :], o_planes[:, LAST, :])
+
+        o_codes = own("o_codes", [P, NQ], U32)
+        o_scales = own("o_scales", [P, NQ], U8)
         words = out_1[0].rearrange("p n t -> p (n t)").bitcast(I32)
-        for h in range(2):
-            cols = slice(h * HALF, (h + 1) * HALF)
-            nc.vector.tensor_copy(o_grp[h][:], o_sb[:, :, cols].rearrange("p j q -> p q j"))
-        for h in range(2):
-            cols = slice(h * HALF, (h + 1) * HALF)
-            nc.vector.quantize_mx(
-                out=o_codes[:, cols].bitcast(FP8X4), scales=o_scales[:, cols], in_=o_grp[h][:].rearrange("p q j -> p (q j)")
-            )
-            nc.sync.dma_start(words[:, cols], o_codes[:, cols].bitcast(I32))
-        for quad in range(4):
-            eng = nc.scalar if quad % 2 else nc.sync
-            eng.dma_start(
+
+        def grouped_quarter(c):
+            return o_grouped[c // 2][:, quarters[c % 2], :]
+
+        def finish_weave(copy, c):
+            weave(copy, grouped_quarter(c)[:, :, 2:4], o_planes[:, 2:4, quarters[c]])
+
+        def quantise_o(c):
+            quantise(o_codes[:, quarters[c]], o_scales[:, quarters[c]], grouped_quarter(c))
+
+        finish_weave(nc.scalar.copy, 3)
+        finish_weave(nc.vector.tensor_copy, 0)
+        finish_weave(nc.vector.tensor_copy, 1)
+        quantise_o(0)
+        finish_weave(nc.vector.tensor_copy, 2)
+        quantise_o(1)
+        nc.sync.dma_start(words[:, halves[0]], o_codes[:, halves[0]].bitcast(I32))
+        quantise_o(2)
+        quantise_o(3)
+        nc.sync.dma_start(words[:, halves[1]], o_codes[:, halves[1]].bitcast(I32))
+        for quad in range(QUADRANTS):
+            queue = nc.scalar if quad % 2 else nc.sync
+            queue.dma_start(
                 out_2[0, 4 * quad : 4 * quad + 4, :].bitcast(I32),
                 o_scales[32 * quad : 32 * quad + 4, :].bitcast(I32),
             )

from contextlib import ExitStack

import concourse.mybir as mybir
from concourse.masks import make_identity

F32 = mybir.dt.float32
BF16 = mybir.dt.bfloat16
I32 = mybir.dt.int32
U32 = mybir.dt.uint32
U16 = mybir.dt.uint16
U8 = mybir.dt.uint8
FP8X4 = mybir.dt.float8_e4m3fn_x4
ACT = mybir.ActivationFunctionType
ALU = mybir.AluOpType

P = 128
PACK = 4
QUADRANTS = 4
SLOTS = 512
NEURONS = 2048
NQ = 512
HALF = NQ // 2
RUN = 4
POOL_BYTES = NEURONS * 4
SECOND_TENANT = 2048
LAST = PACK - 1

TURN_BANKS = (4, 5, 6)
BIAS_BANK = 7
TAIL_BANKS = (3, 7, 5, 6)

FLOPS = 2 * (2 * 512 * SLOTS * NQ)


def tile_attend_plo_mlprelu_topk_kernel(tc, qT, k_words, k_scales, vT, nb, us, offs, out_0, out_1, out_2):
    nc = tc.nc
    halves = [slice(h * HALF, (h + 1) * HALF) for h in range(2)]
    quarters = [slice(c * P, (c + 1) * P) for c in range(NQ // P)]

    with ExitStack() as ctx:
        held = ctx.enter_context(tc.tile_pool(name="held", bufs=1))
        reused = ctx.enter_context(tc.tile_pool(name="reused", bufs=1))
        psum = ctx.enter_context(tc.psum_pool(name="psum", bufs=1))

        def own(name, shape, dtype):
            return held.tile(shape, dtype, name=name, align_bytes=64)

        def placed(name, shape, dtype, offset):
            return reused.tile(shape, dtype, name=name, offset=offset, align_bytes=64)

        def bank(b, shape, name):
            return psum.tile(shape, F32, name=name, tag="bank%d" % b)

        def weave(copy, grouped, planes):
            copy(grouped.rearrange("p (c i) t -> p c t i", i=RUN), planes.rearrange("p t (c i) -> p c t i", i=RUN))

        def quantise(codes, scales, grouped):
            nc.vector.quantize_mx(out=codes.bitcast(FP8X4), scales=scales, in_=grouped.rearrange("p c t -> p (c t)"))

        def product(acc, left, left_scales, right, right_scales):
            nc.tensor.matmul_mx(
                out=acc,
                lhsT=left.bitcast(FP8X4),
                lhsT_scale=left_scales,
                rhs=right.bitcast(FP8X4),
                rhs_scale=right_scales,
                start=True,
                stop=True,
            )

        offsets = held.tile([P, SLOTS // 16], U16, name="offsets")
        nc.sync.dma_start(offsets[:], offs)

        k_scale_pool = own("k_scale_pool", [P, NEURONS], U8)
        nb_pool = own("nb_pool", [P, NEURONS], F32)
        nc.gpsimd.memset(k_scale_pool[:].bitcast(I32), 0)
        nc.vector.memset(nb_pool[0 : P - 1, :], 0.0)

        us_sb = own("us_sb", [P, PACK], F32)
        nc.sync.dma_start(us_sb[:], us[0].rearrange("(p t) o -> p (t o)", t=PACK))
        nc.scalar.dma_start(nb_pool[P - 1 : P, :], nb[0:1, :])
        for quad in range(QUADRANTS):
            queue = nc.sync if quad < QUADRANTS // 2 else nc.scalar
            queue.dma_start(
                k_scale_pool[32 * quad : 32 * quad + 4, :].bitcast(I32),
                k_scales[0, 4 * quad : 4 * quad + 4, :].bitcast(I32),
            )
        q_planes = own("q_planes", [P, PACK, NQ], F32)
        nc.sync.dma_start(q_planes[:], qT[0].rearrange("(p t) q -> p t q", t=PACK))
        k_word_pool = own("k_word_pool", [P, NEURONS], I32)
        nc.sync.dma_start(k_word_pool[:], k_words[0].rearrange("p n t -> p (n t)").bitcast(I32))
        v_rows = vT.rearrange("(p j) n -> p j n", j=PACK)
        v_pool = [placed("v_pool%d" % j, [P, NEURONS], F32, POOL_BYTES * j) for j in range(PACK)]
        for j in range(PACK):
            nc.sync.dma_start(v_pool[j][:], v_rows[:, j, :])

        ident = own("ident", [P, P], F32)
        make_identity(nc, ident[:])

        us_abs = own("us_abs", [P, PACK], F32)
        us_sign = own("us_sign", [P, PACK], F32)
        nc.scalar.activation(us_abs[:], us_sb[:], ACT.Abs)
        nc.scalar.activation(us_sign[:], us_sb[:], ACT.Sign)

        nb_listed = own("nb_listed", [P, SLOTS], F32)
        nc.vector.tensor_copy(nb_listed[:], nb_pool[:].indirect(offsets[:]))
        nb_turned = bank(BIAS_BANK, [P, PACK, P], "nb_turned")
        for t in range(PACK):
            nc.tensor.transpose(nb_turned[:, t, :], nb_listed[:, t:SLOTS:PACK], ident[:])

        k_scales_listed = own("k_scales_listed", [P, SLOTS], U8)
        nc.vector.tensor_copy(k_scales_listed[:], k_scale_pool[:].indirect(offsets[:]))
        bias = own("bias", [P, PACK], F32)
        nc.vector.tensor_tensor(bias[:], nb_turned[:, :, P - 1], us_abs[:], ALU.mult)
        k_scales_dealt = own("k_scales_dealt", [P, PACK, P], U8)
        nc.vector.tensor_copy(
            k_scales_dealt[:].rearrange("p t s -> p s t"), k_scales_listed[:].rearrange("p (s t) -> p s t", t=PACK)
        )

        q_codes = own("q_codes", [P, NQ], U32)
        q_scales = own("q_scales", [P, NQ], U8)
        q_grouped = [own("q_grouped%d" % h, [P, HALF, PACK], BF16) for h in range(2)]
        weave(nc.scalar.copy, q_grouped[0][:], q_planes[:, :, halves[0]])
        weave(nc.vector.tensor_copy, q_grouped[1][:], q_planes[:, :, halves[1]])
        for h in range(2):
            quantise(q_codes[:, halves[h]], q_scales[:, halves[h]], q_grouped[h][:])

        k_words_dealt = own("k_words_dealt", [P, PACK, P], U32)
        nc.vector.tensor_copy(
            k_words_dealt[:].rearrange("p t s -> p s t"), k_word_pool[:].bitcast(U32).indirect(offsets[:])
        )

        y_abs = [own("y_abs%d" % t, [P, NQ], BF16) for t in range(PACK)]
        for t in range(PACK):
            scores = bank(t, [P, NQ], "scores%d" % t)
            product(scores[:], k_words_dealt[:, t, :], k_scales_dealt[:, t, :], q_codes[:], q_scales[:])
            nc.scalar.activation(
                y_abs[t][:], scores[:], ACT.Relu, bias=bias[:, t : t + 1], scale=us_abs[:, t : t + 1]
            )

        v_codes = [placed("v_codes%d" % j, [P, P], U32, POOL_BYTES * (j + 1)) for j in range(LAST)]
        v_codes.append(own("v_codes%d" % LAST, [P, P], U32))
        v_scales = [own("v_scales%d" % j, [P, P], U8) for j in range(PACK)]
        v_grouped = [own("v_grouped%d" % j, [P, P, PACK], BF16) for j in range(LAST)]
        v_grouped.append(placed("v_grouped%d" % LAST, [P, P, PACK], BF16, POOL_BYTES * PACK))

        def gather_and_turn(j):
            listed = own("v_listed%d" % j, [P, SLOTS], BF16)
            nc.vector.tensor_copy(listed[:], v_pool[j][:].indirect(offsets[:]))
            pairs = listed[:].bitcast(F32)
            turned = bank(TURN_BANKS[j % len(TURN_BANKS)], [P, 2, P], "v_turned%d" % j)
            for u in range(2):
                nc.tensor.transpose(turned[:, u, :], pairs[:, u : SLOTS // 2 : 2], ident[:])
            nc.scalar.copy(v_grouped[j][:].bitcast(F32), turned[:].rearrange("p u e -> p e u"))

        def quantise_v(j):
            quantise(v_codes[j][:], v_scales[j][:], v_grouped[j][:])

        gather_and_turn(0)
        y_planes = placed("y_planes", [P, PACK, NQ], BF16, 0)
        for t in range(PACK):
            nc.vector.tensor_scalar(y_planes[:, t, :], y_abs[t][:], us_sign[:, t : t + 1], None, ALU.mult)
        gather_and_turn(1)
        y_grouped = own("y_grouped", [P, NQ, PACK], BF16)
        weave(nc.scalar.copy, y_grouped[:], y_planes[:])
        quantise_v(0)
        gather_and_turn(2)
        y_codes = placed("y_codes", [P, NQ], U32, POOL_BYTES * 2 + SECOND_TENANT)
        y_scales = own("y_scales", [P, NQ], U8)
        quantise(y_codes[:], y_scales[:], y_grouped[:])
        quantise_v(1)

        o_planes = own("o_planes", [P, PACK, NQ], F32)
        out_rows = out_0.rearrange("(p j) q -> p j q", j=PACK)

        def result(j, b, cols):
            acc = bank(b, [P, cols.stop - cols.start], "result%d_%d" % (j, b))
            product(acc[:], v_codes[j][:], v_scales[j][:], y_codes[:, cols], y_scales[:, cols])
            nc.scalar.copy(o_planes[:, j, cols], acc[:])

        def whole_plane(j):
            result(j, j, slice(0, NQ))
            nc.sync.dma_start(out_rows[:, j, :], o_planes[:, j, :])

        whole_plane(0)
        whole_plane(1)
        gather_and_turn(LAST)
        quantise_v(2)

        o_grouped = [placed("o_grouped0", [P, HALF, PACK], BF16, POOL_BYTES * LAST + SECOND_TENANT)]
        weave(nc.vector.tensor_copy, o_grouped[0][:, :, 0:2], o_planes[:, 0:2, halves[0]])
        whole_plane(2)
        quantise_v(LAST)
        o_grouped.append(placed("o_grouped1", [P, HALF, PACK], BF16, POOL_BYTES * PACK))
        weave(nc.vector.tensor_copy, o_grouped[1][:, :, 0:2], o_planes[:, 0:2, halves[1]])

        for c in range(len(quarters)):
            result(LAST, TAIL_BANKS[c], quarters[c])
        nc.sync.dma_start(out_rows[:, LAST, :], o_planes[:, LAST, :])

        o_codes = own("o_codes", [P, NQ], U32)
        o_scales = own("o_scales", [P, NQ], U8)
        words = out_1[0].rearrange("p n t -> p (n t)").bitcast(I32)

        def grouped_quarter(c):
            return o_grouped[c // 2][:, quarters[c % 2], :]

        def finish_weave(copy, c):
            weave(copy, grouped_quarter(c)[:, :, 2:4], o_planes[:, 2:4, quarters[c]])

        def quantise_o(c):
            quantise(o_codes[:, quarters[c]], o_scales[:, quarters[c]], grouped_quarter(c))

        finish_weave(nc.scalar.copy, 3)
        finish_weave(nc.vector.tensor_copy, 0)
        finish_weave(nc.vector.tensor_copy, 1)
        quantise_o(0)
        finish_weave(nc.vector.tensor_copy, 2)
        quantise_o(1)
        nc.sync.dma_start(words[:, halves[0]], o_codes[:, halves[0]].bitcast(I32))
        quantise_o(2)
        quantise_o(3)
        nc.sync.dma_start(words[:, halves[1]], o_codes[:, halves[1]].bitcast(I32))
        for quad in range(QUADRANTS):
            queue = nc.scalar if quad % 2 else nc.sync
            queue.dma_start(
                out_2[0, 4 * quad : 4 * quad + 4, :].bitcast(I32),
                o_scales[32 * quad : 32 * quad + 4, :].bitcast(I32),
            )
